import numpy as np, ml_dtypes
CORES = [24,48,72,152,176,200]
N = 6
import mx_ref
NC, G = 256, 4
CNT = [[56,0,0,80,0,120],[112,0,0,0,96,48],[72,80,24,80,0,0],[0,32,32,104,0,88],[16,64,56,64,40,16],[32,64,64,24,40,32]]
OFF = [[sum(c[:e]) for e in range(N + 1)] for c in CNT]
TOT = [sum(c[e] for c in CNT) for e in range(N)]
C = np.float32(0.031)
BF = ml_dtypes.bfloat16
def cut(t, i, w=512):
    return t[:, w * i:w * i + w]
def tile(rs):
    return np.stack(rs, axis=2).reshape(128, -1).astype(BF)
def layer(w, X):
    out = []
    for i in range(G):
        for t in range(len(X)):
            p = mx_ref.matmul(mx_ref.quantize(cut(w, len(X) * i + t)), X[t])
            z = p if t == 0 else z + p
        out.append(z)
    return out
def act(Z):
    return [np.maximum(z, 0) * C for z in Z]
def setup_inputs(rng):
    def f(*shape):
        return mx_ref.flush((rng.standard_normal(shape, dtype=np.float32) * np.exp2(rng.integers(-2, 3, shape[:-1] + (1,)))).astype(BF))
    return {"x": f(N, 128, 4 * NC), "w1": f(N, 128, G * 512), "w2": f(N, 128, 512)}
def setup_inputs_blocks(rng):
    d = setup_inputs(rng)
    for k in ("x", "w1", "w2"): d[k] = mx_ref.spread(d[k], rng, 4)
    return d
def setup_inputs_wide(rng):
    d = setup_inputs(rng)
    for k in ("x", "w1", "w2"): d[k] = mx_ref.flush((d[k].astype(np.float32) * np.exp2(rng.integers(-8, 9, (N, 1, 1))).astype(np.float32)).astype(BF))
    return d
def setup_inputs_zeros(rng):
    d = setup_inputs(rng); v = d["x"].reshape(N, 128, -1, 4).copy()
    v[np.broadcast_to((rng.random((N, 1, v.shape[2], 1)) < 0.33), v.shape)] = 0
    d["x"] = v.reshape(d["x"].shape)
    return d
def reference(x, w1, w2):
    y = np.full((N, 128, max(TOT)), np.nan, np.float32)
    for e in range(N):
        t = np.concatenate([x[j][:, 4 * OFF[j][e]:4 * OFF[j][e + 1]] for j in range(N)], axis=1)
        y[e][:, :TOT[e]] = mx_ref.matmul(mx_ref.quantize(w2[e]), mx_ref.quantize(tile(act(layer(w1[e], [mx_ref.quantize(t)])))))
    return {"y": y}

from concourse.bass import DstId, RemoteDMATransfer
from concourse.mybir import dt, AluOpType, ActivationFunctionType

NSIM = 256
NCOL = 256
HALF = 128
ACT_C = 0.031
NE_ON = 8
NE_OFF = 8
NREL = 2
LATE_AFTER = 6
WB = 400
WH = 392

SCRATCH = {
    "xt": ("sbuf", [128, 4 * NCOL], "bfloat16"),
    "w1t": ("sbuf", [128, 2048], "bfloat16"),
    "w2t": ("sbuf", [128, 512], "bfloat16"),
    "xq": ("sbuf", [128, NCOL], "float8_e4m3fn_x4"),
    "xs": ("sbuf", [128, NCOL], "uint8"),
    "w1q": ("sbuf", [128, 512], "float8_e4m3fn_x4"),
    "w1s": ("sbuf", [128, 512], "uint8"),
    "w2q": ("sbuf", [128, 128], "float8_e4m3fn_x4"),
    "w2s": ("sbuf", [128, 128], "uint8"),
    "bq": ("sbuf", [128, WB], "float8_e4m3fn_x4"),
    "bs": ("sbuf", [128, WB], "uint8"),
    "ht": ("sbuf", [128, 4 * WH], "bfloat16"),
    "hq": ("sbuf", [128, WH], "float8_e4m3fn_x4"),
    "hs": ("sbuf", [128, WH], "uint8"),
    "yt": ("sbuf", [128, 352], "float32"),
    "z": ("psum", [128, 4096], "float32"),
}
SEMAPHORES = ["sx1", "sx2", "sw1", "sw2", "qx1", "qx2", "qo", "qw1", "qw2", "early", "late", "rp", "rc", "lsem", "st"] + [
    "%s%d" % (n, c) for c in range(2) for n in ("m0_", "m1_", "m2_", "m3_", "a", "hd", "yy", "cp")]

_CACHE = {}


def _groups(order, pos, cnt):
    if len(order) <= NREL:
        return [[e] for e in order]
    best = None
    for k in range(1, len(order)):
        gs = [order[:k], order[k:]]
        key = (max(len(q) for q in gs), sum(pos[q[-1]] + cnt[q[-1]] - pos[q[0]] for q in gs))
        if best is None or key < best[0]:
            best = (key, gs)
    return best[1]


def _batches(q, cnt):
    out = []
    for e in q:
        if out and len(out[-1]) < 2 and cnt[out[-1][0]] == cnt[e]:
            out[-1].append(e)
        else:
            out.append([e])
    return out


def _pieces(lo, hi, s):
    out, c = [], lo
    while c < hi:
        xc = (c + s) % NCOL
        w = min(hi - c, NCOL - xc)
        out.append((c, xc, w))
        c += w
    return out


def _plan(CNT, cores, topo):
    n = len(cores)
    off = [[sum(c[:e]) for e in range(n + 1)] for c in CNT]
    tot = [sum(c[e] for c in CNT) for e in range(n)]
    ypos = [[sum(CNT[i][e] for i in range(j)) for e in range(n)] for j in range(n)]
    snd = []
    for j in range(n):
        cj, cnt = cores[j], CNT[j]
        dests = [e for e in range(n) if e != j and cnt[e] > 0]
        cross = [e for e in dests if not topo.may_write(cj, cores[e])]
        direct = sorted([e for e in dests if e not in cross], key=lambda e: -tot[e])
        prio = cross if cross else direct
        best = None
        for s in sorted(set(off[j][e] for e in range(n) if cnt[e] > 0)):
            pos = dict((e, (off[j][e] - s) % NCOL) for e in range(n) if cnt[e] > 0)
            order = sorted(prio, key=lambda e: pos[e])
            gs = _groups(order, pos, cnt) if cross else [[e] for e in order]
            wins = [(pos[q[0]], pos[q[-1]] + cnt[q[-1]]) for q in gs]
            key = (wins[0][1] > HALF, s + HALF > NCOL, sum(b - a for a, b in wins), len(_pieces(0, HALF, s)) + len(_pieces(HALF, NCOL, s)))
            if best is None or key < best[0]:
                best = (key, s, pos, gs, wins)
        _, s, pos, gs, wins = best
        relays = []
        if cross:
            taken = []
            for q, w in zip(gs, wins):
                cand = [c for c in range(NSIM) if c not in cores and c not in taken and topo.host(c) == topo.host(cj)
                        and topo.chip(c) == topo.chip(cj) and all(topo.may_write(c, cores[e]) for e in q)]
                cand.sort(key=lambda c: (topo.die(c) != topo.die(cj), c))
                taken.append(cand[0])
                relays.append((cand[0], q, w))
        snd.append({"s": s, "pos": pos, "relays": relays, "direct": direct, "cross": cross, "slow": []})
    lcols = [sum(CNT[j][e] for j in range(n) if e in snd[j]["cross"]) for e in range(n)]
    for j in range(n):
        d = snd[j]["direct"]
        d.sort(key=lambda e: (CNT[e][e] > 0 and lcols[e] + CNT[j][e] <= HALF, -tot[e]))
        for i, e in enumerate(d):
            if 2 * len(snd[j]["relays"]) + 2 * (i + 1) > LATE_AFTER and CNT[e][e] > 0 and lcols[e] + CNT[j][e] <= HALF:
                snd[j]["slow"].append(e)
                lcols[e] += CNT[j][e]
    rcv = []
    for e in range(n):
        late = [j for j in range(n) if j != e and CNT[j][e] > 0 and (e in snd[j]["cross"] or e in snd[j]["slow"])]
        direct = [j for j in range(n) if j != e and CNT[j][e] > 0 and j not in late]
        own = CNT[e][e]
        lw, dw = sum(CNT[j][e] for j in late), sum(CNT[j][e] for j in direct)
        at, win = {}, None
        if own == 0:
            c = 0
            for j in sorted(late + direct):
                at[j] = c
                c += CNT[j][e]
            chunks = [(0, c, sorted(late + direct))]
        else:
            p0 = snd[e]["pos"][e]
            if p0 + HALF <= NCOL:
                c = c0 = (-(lw + dw)) % 16
                for j in late + [j for j in direct if j > e] + [j for j in direct if j < e]:
                    at[j] = c
                    c += CNT[j][e]
                at[e] = c
                win = (p0, c)
                chunks = [(c0 + lw, max(HALF, dw + own), direct + [e]), (c0, max(HALF, lw), late)]
            else:
                win = (p0 + own - HALF, 0)
                at[e] = HALF - own
                c = HALF
                for j in [j for j in direct if j > e] + [j for j in direct if j < e] + late:
                    at[j] = c
                    c += CNT[j][e]
                k1, k2 = max(HALF, dw + own), max(HALF, lw)
                chunks = [(HALF + dw - k1, k1, direct + [e]), (c - k2, k2, late)]
            if not late:
                chunks = chunks[:1]
        ch = []
        for st, k, js in chunks:
            runs = []
            for j in sorted(js, key=lambda j: at[j]):
                a, y0, w = at[j] - st, ypos[j][e], CNT[j][e]
                if runs and runs[-1][0] + runs[-1][2] == a and runs[-1][1] + runs[-1][2] == y0:
                    runs[-1] = (runs[-1][0], runs[-1][1], runs[-1][2] + w)
                else:
                    runs.append((a, y0, w))
            ch.append((st, k, runs))
        if len(ch) == 2:
            f0 = min(r[1] for r in ch[1][2])
            f1 = max(r[1] + r[2] for r in ch[1][2])
            stores = [[(a, b) for a, b in ((0, f0), (f1, tot[e])) if b > a], [(f0, f1)]]
        else:
            stores = [[(0, tot[e])]]
        ne = {}
        for j in late + direct:
            ne[j] = NE_OFF
            for rc, q, w in snd[j]["relays"]:
                for batch in _batches(q, CNT[j]):
                    if e in batch:
                        ne[j] = NE_OFF // len(batch)
        rcv.append({"at": at, "win": win, "chunks": ch, "stores": stores,
                    "nlate": sum(2 * ne[j] for j in late), "ndirect": sum(2 * ne[j] for j in direct)})
    return snd, rcv


def _low(mask, k):
    out, b = 0, 1
    while k > 0:
        if mask & b:
            out |= b
            k -= 1
        b <<= 1
    return out


def _views(T, kind, src_lo, dst_lo, w, to_b):
    if kind == "q":
        return T.xq[:, src_lo:src_lo + w].bitcast(dt.uint8), (T.bq if to_b else T.xq)[:, dst_lo:dst_lo + w].bitcast(dt.uint8)
    return T.xs[:, src_lo:src_lo + w], (T.bs if to_b else T.xs)[:, dst_lo:dst_lo + w]


def _send(g, T, topo, core, dst, kind, src_lo, dst_lo, w, to_b, sem):
    same = topo.host(core) == topo.host(dst) and topo.chip(core) == topo.chip(dst)
    ne = NE_ON if same else NE_OFF
    rid, pid = topo.addr(dst, core)
    src, out = _views(T, kind, src_lo, dst_lo, w, to_b)
    g.remote_dma(out_ap=out, in_ap=src, remote_sem=sem, local_sem=T.sem.lsem, pid=pid, routing_id=rid,
                 dma_engine_mask=_low(topo.mask(core, dst), ne))
    return ne


def _send_fused(g, T, topo, core, items, kind, sem):
    ne, trs, used = NE_OFF // len(items), [], 0
    for dst, src_lo, dst_lo, w in items:
        rid, pid = topo.addr(dst, core)
        src, out = _views(T, kind, src_lo, dst_lo, w, True)
        m = _low(topo.mask(core, dst) & ~used, ne)
        used |= m
        trs.append(RemoteDMATransfer(dst_ids=[DstId(rid=rid, pnc=pid)], dma_engine_mask=m, remote_sem=sem, src=src, dst=out))
    g.remote_dma_fused(trs, local_sem=T.sem.lsem)
    return ne * len(items)


def rank_program(g, core, T, topo):
    CNT = T.tables["CNT"]
    cores = list(T.cores)
    if "p" not in _CACHE:
        _CACHE["p"] = _plan(CNT, cores, topo)
    snd, rcv = _CACHE["p"]
    S = T.sem
    rank = T.rank_of(core)

    if rank is None:
        for j in range(len(cores)):
            for rc, q, w in snd[j]["relays"]:
                if rc != core:
                    continue
                sent = 0
                for kind, sem in (("s", S.rp), ("q", S.rc)):
                    g.wait_ge(sem, NE_ON)
                    for batch in _batches(q, CNT[j]):
                        items = [(cores[e], snd[j]["pos"][e], rcv[e]["at"][j], CNT[j][e]) for e in batch]
                        if len(items) == 1:
                            sent += _send(g, T, topo, core, items[0][0], kind, items[0][1], items[0][2], items[0][3], True, S.late)
                        else:
                            sent += _send_fused(g, T, topo, core, items, kind, S.late)
                g.wait_ge(S.lsem, sent)
        return

    me, R = snd[rank], rcv[rank]
    s = me["s"]

    p1, p2 = _pieces(0, HALF, s), _pieces(HALF, NCOL, s)
    for c, xc, w in p1:
        g.sync.dma_start(T.xt[:, 4 * c:4 * (c + w)], T.x[:, 4 * xc:4 * (xc + w)]).then_inc(S.sx1, 16)
    for i, (c, xc, w) in enumerate(p2):
        (g.scalar if i == 0 else g.sync).dma_start(T.xt[:, 4 * c:4 * (c + w)], T.x[:, 4 * xc:4 * (xc + w)]).then_inc(S.sx2, 16)
    g.sync.dma_start(T.w1t[:], T.w1[:]).then_inc(S.sw1, 16)
    g.sync.dma_start(T.w2t[:], T.w2[:]).then_inc(S.sw2, 16)

    v = g.vector
    v.wait_ge(S.sx1, 16 * len(p1))
    v.quantize_mx(T.xq[:, 0:HALF], T.xs[:, 0:HALF], T.xt[:, 0:4 * HALF]).then_inc(S.qx1, 1)
    v.wait_ge(S.sx2, 16 * len(p2))
    v.quantize_mx(T.xq[:, HALF:NCOL], T.xs[:, HALF:NCOL], T.xt[:, 4 * HALF:4 * NCOL]).then_inc(S.qx2, 1)
    if R["win"] is not None:
        a, b = R["win"]
        v.quantize_mx(T.bq[:, b:b + HALF], T.bs[:, b:b + HALF], T.xt[:, 4 * a:4 * (a + HALF)]).then_inc(S.qo, 1)
    v.wait_ge(S.sw1, 16)
    v.quantize_mx(T.w1q[:], T.w1s[:], T.w1t[:]).then_inc(S.qw1, 1)
    v.wait_ge(S.sw2, 16)
    v.quantize_mx(T.w2q[:], T.w2s[:], T.w2t[:]).then_inc(S.qw2, 1)

    jobs = [(rc, "s", w[0], w[0], w[1] - w[0], False, S.rp) for rc, q, w in me["relays"]]
    jobs += [(rc, "q", w[0], w[0], w[1] - w[0], False, S.rc) for rc, q, w in me["relays"]]
    for e in me["direct"]:
        for kind in ("s", "q"):
            jobs.append((cores[e], kind, me["pos"][e], rcv[e]["at"][rank], CNT[rank][e], True, S.late if e in me["slow"] else S.early))
    have, sent = [False, False], 0
    for dst, kind, lo, dlo, w, to_b, sem in jobs:
        if lo < HALF and not have[0]:
            g.wait_ge(S.qx1, 1)
            have[0] = True
        if lo + w > HALF and not have[1]:
            g.wait_ge(S.qx2, 1)
            have[1] = True
        sent += _send(g, T, topo, core, dst, kind, lo, dlo, w, to_b, sem)
    for i, sem in enumerate((S.qx1, S.qx2)):
        if not have[i]:
            g.wait_ge(sem, 1)
    g.wait_ge(S.lsem, sent)

    t, sc = g.tensor, g.scalar
    t.wait_ge(S.qw1, 1)
    if R["win"] is not None:
        t.wait_ge(S.qo, 1)
    nch, hb, nst = len(R["chunks"]), 0, 0
    for c, (st, k, runs) in enumerate(R["chunks"]):
        if c == 0 and R["ndirect"]:
            t.wait_ge(S.early, R["ndirect"])
        if c == nch - 1 and R["nlate"]:
            t.wait_ge(S.late, R["nlate"])
        for b in range(4):
            bank = 512 * (4 * c + b)
            t.matmul_mx(T.z[:, bank:bank + k], T.w1q[:, 128 * b:128 * b + 128], T.w1s[:, 128 * b:128 * b + 128],
                        T.bq[:, st:st + k], T.bs[:, st:st + k], True, True).then_inc(S["m%d_%d" % (b, c)], 1)
        for b in range(4):
            bank = 512 * (4 * c + b)
            out = T.ht[:, 4 * hb + b:4 * (hb + k):4]
            if b % 2 == 0:
                sc.wait_ge(S["m%d_%d" % (b, c)], 1)
                sc.activation(out, T.z[:, bank:bank + k], ActivationFunctionType.Relu, scale=ACT_C).then_inc(S["a%d" % c], 1)
            else:
                v.wait_ge(S["m%d_%d" % (b, c)], 1)
                v.tensor_scalar(out, T.z[:, bank:bank + k], 0.0, ACT_C, AluOpType.max, AluOpType.mult).then_inc(S["a%d" % c], 1)
        v.wait_ge(S["a%d" % c], 4)
        v.quantize_mx(T.hq[:, hb:hb + k], T.hs[:, hb:hb + k], T.ht[:, 4 * hb:4 * (hb + k)]).then_inc(S["hd%d" % c], 1)
        if c == 0:
            t.wait_ge(S.qw2, 1)
        t.wait_ge(S["hd%d" % c], 1)
        bank = 512 * 4 * c
        t.matmul_mx(T.z[:, bank:bank + k], T.w2q[:], T.w2s[:], T.hq[:, hb:hb + k], T.hs[:, hb:hb + k], True, True).then_inc(S["yy%d" % c], 1)
        v.wait_ge(S["yy%d" % c], 1)
        for a, y0, w in runs:
            v.tensor_copy(T.yt[:, y0:y0 + w], T.z[:, bank + a:bank + a + w]).then_inc(S["cp%d" % c], 1)
        g.sync.wait_ge(S["cp%d" % c], len(runs))
        for y0, y1 in R["stores"][c]:
            g.sync.dma_start(T.y[:, y0:y1], T.yt[:, y0:y1]).then_inc(S.st, 16)
            nst += 1
        hb += k
    g.sync.wait_ge(S.st, 16 * nst)
